import numpy as np
import ml_dtypes


def mxq(x, axis, fmt="e4m3"):
    dtype, down = {"e4m3": (ml_dtypes.float8_e4m3fn, 7), "e5m2": (ml_dtypes.float8_e5m2, 14)}[fmt]
    v = np.moveaxis(np.asarray(x, np.float32).astype(ml_dtypes.bfloat16).astype(np.float64), axis, -1)
    blocks = v.reshape(v.shape[:-1] + (-1, 32))
    amax = np.abs(blocks).max(-1, keepdims=True)
    byte = np.maximum(np.where(amax > 0, np.frexp(amax)[1] - 1 + 127, 0) - down, 1)
    scale = np.exp2(byte - 127.0)
    codes = (blocks / scale).astype(np.float32).astype(dtype).astype(np.float64)
    return np.moveaxis((codes * scale).reshape(v.shape), -1, axis)


WIDE = False


def mx_kscale(k):
    if not WIDE:
        return np.ones(k)
    levels = np.array([10, -10, 5, -5, 0])
    if k % 512:
        return np.exp2(np.random.permutation(np.resize(levels, k // 32))).repeat(32)
    a = np.empty((k // 512, 16))
    for p in range(k // 512):
        a[p, :8] = np.random.permutation(np.resize(levels, 8))
        for g in range(8):
            far = levels[np.abs(levels - a[p, g]) >= 10]
            a[p, g + 8] = far[np.random.randint(len(far))]
    return np.exp2(a.ravel()).repeat(32)


def f64(x):
    return np.asarray(x).astype(np.float64)


def striped(idx):
    return np.tile(idx.reshape(-1, 16).T, (8, 1)).astype(np.uint16)


def unstriped(offs):
    return offs[:16].T.reshape(-1).astype(np.int64)


E2M1 = np.array([0.0, 0.5, 1.0, 1.5, 2.0, 3.0, 4.0, 6.0, -0.0, -0.5, -1.0, -1.5, -2.0, -3.0, -4.0, -6.0])


def pack_weight(w, fmt):
    k, n = w.shape
    w = f64(np.asarray(w, np.float32).astype(ml_dtypes.bfloat16)).reshape(k // 32, 32, n)
    amax = np.abs(w).max(1)
    if fmt == "e4m3":
        byte = np.frexp(amax)[1] - 1 + 127 - 7
    else:
        mant, ex = np.frexp(amax / 6.0)
        byte = np.where(mant > 0.5, ex, ex - 1) + 127
    byte = np.clip(np.where(amax > 0, byte, 1), 1, 254)
    scaled = (w * np.exp2(127.0 - byte)[:, None, :]).reshape(k, n).astype(np.float32)
    by_word = np.ascontiguousarray(scaled.reshape(k // 512, 128, 4, n).transpose(0, 1, 3, 2))
    if fmt == "e4m3":
        words = by_word.astype(ml_dtypes.float8_e4m3fn).view(np.uint8)
    else:
        c = by_word.astype(ml_dtypes.float4_e2m1fn).view(np.uint8) & 0xF
        words = (c[..., 0::2] | (c[..., 1::2] << 4)).reshape(k // 512, 128, 2 * n)
    return np.ascontiguousarray(words), np.ascontiguousarray(byte.astype(np.uint8).reshape(k // 512, 16, n))


def unpack_weight(words, scales, fmt):
    g, _, n = scales.shape
    words = np.ascontiguousarray(words).reshape(g, 128, n, -1)
    if fmt == "e4m3":
        vals = words.view(ml_dtypes.float8_e4m3fn).astype(np.float64)
    else:
        nib = np.empty((g, 128, n, 4), np.uint8)
        nib[..., 0::2] = words & 0xF
        nib[..., 1::2] = words >> 4
        vals = E2M1[nib]
    vals = vals * np.repeat(np.exp2(scales.astype(np.float64) - 127.0), 8, axis=1)[..., None]
    return vals.transpose(0, 1, 3, 2).reshape(g * 512, n)


def gelu(v):
    return 0.5 * v * (1.0 + np.tanh(np.sqrt(2.0 / np.pi) * (v + 0.044715 * v**3)))


K, T, S, H, T3, S2, P = 1024, 4096, 1024, 1024, 2048, 512, 512

def setup_inputs():
    n = np.random.standard_normal
    s = mx_kscale(K)[:, None]
    u = mx_kscale(H)[:, None]
    d = {}
    marks = n((K, T)) * s * np.exp(0.5 * n(T))[None, :]
    d["tab_words"], d["tab_scales"] = pack_weight(marks, "e4m3")
    d["offs"] = striped(np.random.permutation(T)[:S])
    d["tab2_words"], d["tab2_scales"] = pack_weight(n((H, T3)) / u / H ** 0.5, "e4m3")
    d["offs2"] = striped(np.random.permutation(T3)[:S2])
    d["pos1"] = striped(np.random.permutation(S)[:P])
    d["pos2"] = striped(np.random.permutation(S)[:P])
    d["w1"] = (1.2 * n((K, H)) / s / K ** 0.5).astype(np.float32)
    d["w4_words"], d["w4_scales"] = pack_weight(1.2 * n((K, H)) / s / K ** 0.5, "e2m1")
    d["gain"] = (np.exp(0.3 * n(H)) * u[:, 0]).astype(np.float32)
    d["habit"] = np.exp(0.4 * n(S2)).astype(np.float32)
    return d

def reference(tab_words, tab_scales, offs, tab2_words, tab2_scales, offs2, pos1, pos2,
              w1, w4_words, w4_scales, gain, habit):
    v = unpack_weight(tab_words, tab_scales, "e4m3")[:, unstriped(offs)]
    w4 = unpack_weight(w4_words, w4_scales, "e2m1")
    a = mxq(f64(w1), 0, "e4m3").T @ v
    b = w4.T @ v
    sq = np.square(np.concatenate([a, b], axis=0))
    h = f64(gain)[:, None] * np.sqrt(sq[:H] + sq[H:] + 1.0)
    hq = mxq(h, 0, "e4m3")
    v2 = unpack_weight(tab2_words, tab2_scales, "e4m3")[:, unstriped(offs2)]
    e = v2.T @ hq
    gap = e[:, unstriped(pos1)] - e[:, unstriped(pos2)]
    return f64(habit)[:, None] * gap

@@ -1,0 +1,254 @@
+from contextlib import ExitStack
+
+import concourse.mybir as mybir
+
+K, T, S, H, T3, S2, NP = 1024, 4096, 1024, 1024, 2048, 512, 512
+FLOPS = 2 * (2 * K * H * S) + 2 * H * S2 * S
+
+F32 = mybir.dt.float32
+BF16 = mybir.dt.bfloat16
+I32 = mybir.dt.int32
+U32 = mybir.dt.uint32
+U16 = mybir.dt.uint16
+U8 = mybir.dt.uint8
+FP8X4 = mybir.dt.float8_e4m3fn_x4
+FP4X4 = mybir.dt.float4_e2m1fn_x4
+ACT = mybir.ActivationFunctionType
+ALU = mybir.AluOpType
+
+P = 128
+
+
+def tile_list_ballot_scanner_gap_kernel(
+    tc, tab_words, tab_scales, offs, tab2_words, tab2_scales, offs2, pos1, pos2,
+    w1, w4_words, w4_scales, gain, habit, out,
+):
+    nc = tc.nc
+    with ExitStack() as ctx:
+        keep = ctx.enter_context(tc.tile_pool(name="keep", bufs=1))
+        ring = ctx.enter_context(tc.tile_pool(name="ring", bufs=2))
+        psum = ctx.enter_context(tc.psum_pool(name="psum", bufs=2))
+
+        tab_s = keep.tile([P, T], U8, name="tab_s", align_bytes=64)
+        w4_s = keep.tile([P, 2, H], U8, name="w4_s", align_bytes=64)
+        tab2_s = keep.tile([P, T3], U8, name="tab2_s", align_bytes=64)
+        v_s1 = keep.tile([P, S], U8, name="v_s1", align_bytes=64)
+        warm = keep.tile([P, 2], F32, name="warm")
+        nc.vector.memset(tab_s[:].bitcast(I32), 0)
+        nc.vector.memset(w4_s[:].rearrange("p a n -> p (a n)").bitcast(I32), 0)
+        nc.vector.memset(warm[:, 0:1], 1.0)
+        nc.scalar.activation(out=warm[:, 1:2], in_=warm[:, 0:1], func=ACT.Sqrt)
+        nc.vector.memset(tab2_s[:].bitcast(I32), 0)
+        nc.vector.memset(v_s1[:].bitcast(I32), 0)
+
+        idx = keep.tile([P, S // 16], U16, name="idx")
+        nc.sync.dma_start(idx[:], offs)
+        for q in range(4):
+            nc.gpsimd.dma_start(
+                tab_s[32 * q : 32 * q + 8, :].bitcast(I32),
+                tab_scales[:, 4 * q : 4 * q + 4, :].bitcast(I32),
+            )
+        w4_w = keep.tile([P, 2, 2 * H], U8, name="w4_w", align_bytes=64)
+        nc.sync.dma_start(w4_w[:].bitcast(I32), w4_words.rearrange("a p n -> p a n").bitcast(I32))
+        tab_w = []
+        for a in range(2):
+            tab_w.append(keep.tile([P, T], I32, name="tab_w%d" % a, align_bytes=64))
+        nc.sync.dma_start(tab_w[0][:], tab_words[0].rearrange("p t i -> p (t i)").bitcast(I32))
+        for q in range(4):
+            nc.sync.dma_start(
+                w4_s[32 * q : 32 * q + 4, :, :].bitcast(I32),
+                w4_scales[:, 4 * q : 4 * q + 4, :].rearrange("a r n -> r a n").bitcast(I32),
+            )
+        nc.sync.dma_start(tab_w[1][:], tab_words[1].rearrange("p t i -> p (t i)").bitcast(I32))
+        g = keep.tile([P, 2, 4], F32, name="g")
+        nc.gpsimd.dma_start(g[:], gain.rearrange("(b p t) -> p b t", b=2, t=4))
+        w1_raw = {}
+        for b in range(2):
+            for a in range(2):
+                w1_raw[b, a] = keep.tile([P, 4, 512], F32, name="w1_raw%d%d" % (b, a))
+                nc.sync.dma_start(
+                    w1_raw[b, a][:],
+                    w1[512 * a : 512 * (a + 1), 512 * b : 512 * (b + 1)].rearrange("(p j) c -> p j c", j=4),
+                )
+        for q in range(4):
+            nc.gpsimd.dma_start(
+                tab2_s[32 * q : 32 * q + 8, :].bitcast(I32),
+                tab2_scales[:, 4 * q : 4 * q + 4, :].bitcast(I32),
+            )
+        idx2 = keep.tile([P, S2 // 16], U16, name="idx2")
+        nc.sync.dma_start(idx2[:], offs2)
+        tab2_w = []
+        for a in range(2):
+            tab2_w.append(keep.tile([P, T3], I32, name="tab2_w%d" % a, align_bytes=64))
+            nc.sync.dma_start(tab2_w[a][:], tab2_words[a].rearrange("p t i -> p (t i)").bitcast(I32))
+        p1 = keep.tile([P, NP // 16], U16, name="p1")
+        nc.sync.dma_start(p1[:], pos1)
+        p2 = keep.tile([P, NP // 16], U16, name="p2")
+        nc.sync.dma_start(p2[:], pos2)
+        hab = keep.tile([P, 4], F32, name="hab")
+        with nc.allow_non_contiguous_dma(reason="one factor a partition"):
+            nc.sync.dma_start(hab[:], habit.rearrange("(c p) -> p c", p=P))
+
+        v_s0 = keep.tile([P, S], U8, name="v_s0", align_bytes=64)
+        nc.vector.tensor_copy(v_s0[:], tab_s[:].indirect(idx[:]))
+        nc.scalar.dma_start(v_s1[0:124, :].bitcast(I32), v_s0[4:128, :].bitcast(I32))
+        v_s = [v_s0, v_s1]
+
+        w4p, w4ps = [], []
+
+        def deal_w4(b):
+            wp = keep.tile([P, 2, 4, 256], U8, name="w4p%d" % b, align_bytes=64)
+            nc.vector.tensor_copy(
+                wp[:].bitcast(U16),
+                w4_w[:, :, 1024 * b : 1024 * (b + 1)].bitcast(U16).rearrange("p a (m t) -> p a t m", t=4),
+            )
+            ws = keep.tile([P, 2, 4, 128], U8, name="w4ps%d" % b, align_bytes=64)
+            nc.vector.tensor_copy(
+                ws[:], w4_s[:, :, 512 * b : 512 * (b + 1)].rearrange("p a (m t) -> p a t m", t=4)
+            )
+            w4p.append(wp)
+            w4ps.append(ws)
+
+        v = {}
+
+        def gather_v(a, h):
+            v[a, h] = keep.tile([P, 512], U32, name="v%d%d" % (a, h), align_bytes=64)
+            nc.vector.tensor_copy(v[a, h][:], tab_w[a][:].bitcast(U32).indirect(idx[:, 32 * h : 32 * (h + 1)]))
+
+        deal_w4(0)
+        gather_v(0, 0)
+        gather_v(0, 1)
+        gather_v(1, 0)
+        gather_v(1, 1)
+        deal_w4(1)
+
+        g2 = keep.tile([P, 2, 4], F32, name="g2")
+        nc.vector.tensor_tensor(g2[:], g[:], g[:], ALU.mult)
+        sgn = []
+        for b in range(2):
+            sgn.append(keep.tile([P, 512, 4], BF16, name="sgn%d" % b, align_bytes=64))
+            nc.scalar.activation(
+                out=sgn[b][:], in_=g[:, b : b + 1, :].to_broadcast([P, 512, 4]), func=ACT.Sign
+            )
+
+        w1q, w1s = {}, {}
+
+        def quant_w1(b, a):
+            wb = ring.tile([P, 4, 128, 4], BF16, name="wb", align_bytes=64)
+            nc.vector.tensor_copy(
+                wb[:].rearrange("p t m j -> p m j t"),
+                w1_raw[b, a][:].rearrange("p j (m t) -> p m j t", t=4),
+            )
+            w1q[b, a] = keep.tile([P, 512], U32, name="w1q%d%d" % (b, a), align_bytes=64)
+            w1s[b, a] = keep.tile([P, 512], U8, name="w1s%d%d" % (b, a), align_bytes=64)
+            nc.vector.quantize_mx(
+                out=w1q[b, a][:].bitcast(FP8X4),
+                scales=w1s[b, a][:],
+                in_=wb[:].rearrange("p t m j -> p (t m j)"),
+            )
+
+        x = {}
+
+        def stage_b(b, h):
+            x[b, h] = keep.tile([P, 4, 512], F32, name="x%d%d" % (b, h))
+            for t in range(4):
+                bank = psum.tile([P, 512], F32, name="bank", bufs=4)
+                for a in range(2):
+                    nc.tensor.matmul_mx(
+                        out=bank[:],
+                        lhsT=w4p[b][:, a, t, :].bitcast(FP4X4),
+                        lhsT_scale=w4ps[b][:, a, t, :],
+                        rhs=v[a, h][:].bitcast(FP8X4),
+                        rhs_scale=v_s[a][:, 512 * h : 512 * (h + 1)],
+                        start=(a == 0),
+                        stop=(a == 1),
+                    )
+                nc.scalar.activation(out=x[b, h][:, t, :], in_=bank[:], func=ACT.Square, scale=g[:, b, t : t + 1])
+
+        hq, hs = {}, {}
+
+        def stage_a(b, h, c0, n):
+            cols = slice(c0, c0 + n)
+            for t in range(4):
+                bank = psum.tile([P, 512], F32, name="bank", bufs=4)
+                for a in range(2):
+                    nc.tensor.matmul_mx(
+                        out=bank[:, 0:n],
+                        lhsT=w1q[b, a][:, 128 * t : 128 * (t + 1)].bitcast(FP8X4),
+                        lhsT_scale=w1s[b, a][:, 128 * t : 128 * (t + 1)],
+                        rhs=v[a, h][:, cols].bitcast(FP8X4),
+                        rhs_scale=v_s[a][:, 512 * h + c0 : 512 * h + c0 + n],
+                        start=(a == 0),
+                        stop=(a == 1),
+                    )
+                sa = ring.tile([P, 512], F32, name="sa", bufs=4)
+                nc.scalar.activation(out=sa[:, 0:n], in_=bank[:, 0:n], func=ACT.Square, scale=g[:, b, t : t + 1])
+                nc.vector.scalar_tensor_tensor(
+                    out=x[b, h][:, t, cols], in0=sa[:, 0:n], scalar=g2[:, b, t : t + 1],
+                    in1=x[b, h][:, t, cols], op0=ALU.add, op1=ALU.add,
+                )
+
+        def stage_h(b, h, c0, n):
+            hb = ring.tile([P, 512, 4], BF16, name="hb", align_bytes=64)
+            nc.scalar.activation(
+                out=hb[:, 0:n, :].rearrange("p (c i) t -> p c t i", i=4),
+                in_=x[b, h][:, :, c0 : c0 + n].rearrange("p t (c i) -> p c t i", i=4),
+                func=ACT.Sqrt,
+            )
+            flat = hb[:, 0:n, :].rearrange("p n t -> p (n t)")
+            nc.vector.tensor_tensor(flat, flat, sgn[b][:, 0:n, :].rearrange("p n t -> p (n t)"), ALU.mult)
+            hq[b, h, c0] = keep.tile([P, n], U32, name="hq%d%d%d" % (b, h, c0), align_bytes=64)
+            hs[b, h, c0] = keep.tile([P, n], U8, name="hs%d%d%d" % (b, h, c0), align_bytes=64)
+            nc.vector.quantize_mx(out=hq[b, h, c0][:].bitcast(FP8X4), scales=hs[b, h, c0][:], in_=flat)
+
+        stage_b(0, 0)
+        stage_b(0, 1)
+        quant_w1(0, 0)
+        quant_w1(0, 1)
+        stage_b(1, 0)
+        stage_a(0, 0, 0, 512)
+        quant_w1(1, 0)
+        stage_b(1, 1)
+        quant_w1(1, 1)
+        stage_a(0, 1, 0, 512)
+        stage_h(0, 0, 0, 512)
+        stage_a(1, 0, 0, 512)
+        stage_h(0, 1, 0, 512)
+
+        v2 = []
+        for a in range(2):
+            v2.append(keep.tile([P, S2], U32, name="v2%d" % a, align_bytes=64))
+            nc.vector.tensor_copy(v2[a][:], tab2_w[a][:].bitcast(U32).indirect(idx2[:]))
+        v2_s = keep.tile([P, S2], U8, name="v2_s", align_bytes=64)
+        nc.vector.tensor_copy(v2_s[:], tab2_s[:].indirect(idx2[:]))
+
+        stage_a(1, 1, 0, 256)
+        stage_h(1, 0, 0, 512)
+        stage_a(1, 1, 256, 256)
+        stage_h(1, 1, 0, 256)
+        stage_h(1, 1, 256, 256)
+
+        pieces = [[(0, 0, 512), (1, 0, 512)], [(0, 0, 512), (1, 0, 256), (1, 256, 256)]]
+        for mt in range(4):
+            m = slice(128 * mt, 128 * (mt + 1))
+            e = keep.tile([P, S], F32, name="e%d" % mt)
+            for h in range(2):
+                bank2 = psum.tile([P, 512], F32, name="e_bank%d" % h)
+                for i, (b, c0, n) in enumerate(pieces[h]):
+                    nc.tensor.matmul_mx(
+                        out=bank2[:, c0 : c0 + n],
+                        lhsT=v2[b][:, m].bitcast(FP8X4),
+                        lhsT_scale=v2_s[4 * b : P, m],
+                        rhs=hq[b, h, c0][:].bitcast(FP8X4),
+                        rhs_scale=hs[b, h, c0][:],
+                        start=(i == 0),
+                        stop=(i == len(pieces[h]) - 1),
+                    )
+                nc.scalar.activation(
+                    out=e[:, 512 * h : 512 * (h + 1)], in_=bank2[:], func=ACT.Copy, scale=hab[:, mt : mt + 1]
+                )
+            second = ring.tile([P, NP], F32, name="second")
+            nc.vector.tensor_copy(second[:], e[:].indirect(p2[:]))
+            gap = ring.tile([P, NP], F32, name="gap", bufs=4)
+            nc.vector.tensor_tensor(gap[:], e[:].indirect(p1[:]), second[:], ALU.subtract)
+            nc.sync.dma_start(out[m, :], gap[:])

@@ -17,6 +17,7 @@ ACT = mybir.ActivationFunctionType
 ALU = mybir.AluOpType
 
 P = 128
+NV = 2
 
 
 def tile_list_ballot_scanner_gap_kernel(
@@ -29,85 +30,101 @@ def tile_list_ballot_scanner_gap_kernel(
         ring = ctx.enter_context(tc.tile_pool(name="ring", bufs=2))
         psum = ctx.enter_context(tc.psum_pool(name="psum", bufs=2))
 
-        tab_s = keep.tile([P, T], U8, name="tab_s", align_bytes=64)
-        w4_s = keep.tile([P, 2, H], U8, name="w4_s", align_bytes=64)
+        share = ctx.enter_context(tc.tile_pool(name="share", bufs=1))
+        KB = 1024
+
+        tab_s = share.tile([P, T], U8, name="tab_s", align_bytes=64, offset=31 * KB)
         tab2_s = keep.tile([P, T3], U8, name="tab2_s", align_bytes=64)
         v_s1 = keep.tile([P, S], U8, name="v_s1", align_bytes=64)
-        warm = keep.tile([P, 2], F32, name="warm")
+        warm = share.tile([P, 32], F32, name="warm", align_bytes=64, offset=9 * KB - 64)
         nc.vector.memset(tab_s[:].bitcast(I32), 0)
-        nc.vector.memset(w4_s[:].rearrange("p a n -> p (a n)").bitcast(I32), 0)
         nc.vector.memset(warm[:, 0:1], 1.0)
-        nc.scalar.activation(out=warm[:, 1:2], in_=warm[:, 0:1], func=ACT.Sqrt)
-        nc.vector.memset(tab2_s[:].bitcast(I32), 0)
         nc.vector.memset(v_s1[:].bitcast(I32), 0)
 
         idx = keep.tile([P, S // 16], U16, name="idx")
         nc.sync.dma_start(idx[:], offs)
-        for q in range(4):
-            nc.gpsimd.dma_start(
-                tab_s[32 * q : 32 * q + 8, :].bitcast(I32),
-                tab_scales[:, 4 * q : 4 * q + 4, :].bitcast(I32),
-            )
+        g = keep.tile([P, 2, 4], F32, name="g")
+        nc.sync.dma_start(g[:], gain.rearrange("(b p t) -> p b t", b=2, t=4))
+        idx2 = keep.tile([P, S2 // 16], U16, name="idx2")
+        nc.sync.dma_start(idx2[:], offs2)
         w4_w = keep.tile([P, 2, 2 * H], U8, name="w4_w", align_bytes=64)
         nc.sync.dma_start(w4_w[:].bitcast(I32), w4_words.rearrange("a p n -> p a n").bitcast(I32))
         tab_w = []
         for a in range(2):
-            tab_w.append(keep.tile([P, T], I32, name="tab_w%d" % a, align_bytes=64))
+            tab_w.append(share.tile([P, T], I32, name="tab_w%d" % a, align_bytes=64, offset=(9 + 24 * a) * KB))
+        p1 = keep.tile([P, NP // 16], U16, name="p1")
+        nc.sync.dma_start(p1[:], pos1)
+        p2 = keep.tile([P, NP // 16], U16, name="p2")
+        nc.sync.dma_start(p2[:], pos2)
+        for r in range(4):
+            nc.sync.dma_start(
+                tab_s[r:P:16, :].bitcast(I32),
+                tab_scales.rearrange("a (q r) n -> r q a n", r=4)[r].bitcast(I32),
+            )
+        nc.scalar.activation(out=warm[:, 1:2], in_=warm[:, 0:1], func=ACT.Sqrt)
+        sgn = []
+
+        def make_sign(b):
+            sgn.append(keep.tile([P, 512, 4], BF16, name="sgn%d" % b, align_bytes=64))
+            nc.scalar.activation(
+                out=sgn[b][:], in_=g[:, b : b + 1, :].to_broadcast([P, 512, 4]), func=ACT.Sign
+            )
+
+        make_sign(0)
+        make_sign(1)
         nc.sync.dma_start(tab_w[0][:], tab_words[0].rearrange("p t i -> p (t i)").bitcast(I32))
+        w4_s = share.tile([P, 2, H], U8, name="w4_s", align_bytes=64, offset=7 * KB)
+        nc.vector.memset(w4_s[:].rearrange("p a n -> p (a n)").bitcast(I32), 0)
         for q in range(4):
             nc.sync.dma_start(
                 w4_s[32 * q : 32 * q + 4, :, :].bitcast(I32),
                 w4_scales[:, 4 * q : 4 * q + 4, :].rearrange("a r n -> r a n").bitcast(I32),
             )
-        nc.sync.dma_start(tab_w[1][:], tab_words[1].rearrange("p t i -> p (t i)").bitcast(I32))
-        g = keep.tile([P, 2, 4], F32, name="g")
-        nc.gpsimd.dma_start(g[:], gain.rearrange("(b p t) -> p b t", b=2, t=4))
-        w1_raw = {}
-        for b in range(2):
-            for a in range(2):
-                w1_raw[b, a] = keep.tile([P, 4, 512], F32, name="w1_raw%d%d" % (b, a))
-                nc.sync.dma_start(
-                    w1_raw[b, a][:],
-                    w1[512 * a : 512 * (a + 1), 512 * b : 512 * (b + 1)].rearrange("(p j) c -> p j c", j=4),
-                )
+        nc.gpsimd.memset(tab2_s[:].bitcast(I32), 0)
         for q in range(4):
             nc.gpsimd.dma_start(
                 tab2_s[32 * q : 32 * q + 8, :].bitcast(I32),
                 tab2_scales[:, 4 * q : 4 * q + 4, :].bitcast(I32),
             )
-        idx2 = keep.tile([P, S2 // 16], U16, name="idx2")
-        nc.sync.dma_start(idx2[:], offs2)
-        tab2_w = []
-        for a in range(2):
-            tab2_w.append(keep.tile([P, T3], I32, name="tab2_w%d" % a, align_bytes=64))
-            nc.sync.dma_start(tab2_w[a][:], tab2_words[a].rearrange("p t i -> p (t i)").bitcast(I32))
-        p1 = keep.tile([P, NP // 16], U16, name="p1")
-        nc.sync.dma_start(p1[:], pos1)
-        p2 = keep.tile([P, NP // 16], U16, name="p2")
-        nc.sync.dma_start(p2[:], pos2)
         hab = keep.tile([P, 4], F32, name="hab")
         with nc.allow_non_contiguous_dma(reason="one factor a partition"):
-            nc.sync.dma_start(hab[:], habit.rearrange("(c p) -> p c", p=P))
+            nc.gpsimd.dma_start(hab[:], habit.rearrange("(c p) -> p c", p=P))
 
-        v_s0 = keep.tile([P, S], U8, name="v_s0", align_bytes=64)
-        nc.vector.tensor_copy(v_s0[:], tab_s[:].indirect(idx[:]))
-        nc.scalar.dma_start(v_s1[0:124, :].bitcast(I32), v_s0[4:128, :].bitcast(I32))
-        v_s = [v_s0, v_s1]
+        w1_raw = {}
+        w1_at = {(0, 0): 25 * KB, (0, 1): 0, (1, 0): 9 * KB, (1, 1): 17 * KB}
+
+        def load_w1(b, a):
+            w1_raw[b, a] = share.tile([P, 4, 512], F32, name="w1_raw%d%d" % (b, a), align_bytes=64, offset=w1_at[b, a])
+            nc.sync.dma_start(
+                w1_raw[b, a][:],
+                w1[512 * a : 512 * (a + 1), 512 * b : 512 * (b + 1)].rearrange("(p j) c -> p j c", j=4),
+            )
+
+        tab2_w = []
+
+        def load_tab2(a):
+            tab2_w.append(share.tile([P, T3], I32, name="tab2_w%d" % a, align_bytes=64, offset=33 * KB + 8 * KB * a))
+            nc.sync.dma_start(tab2_w[a][:], tab2_words[a].rearrange("p t i -> p (t i)").bitcast(I32))
 
         w4p, w4ps = [], []
-
-        def deal_w4(b):
-            wp = keep.tile([P, 2, 4, 256], U8, name="w4p%d" % b, align_bytes=64)
+        for b in range(2):
+            w4p.append(keep.tile([P, 2, 4, 256], U8, name="w4p%d" % b, align_bytes=64))
             nc.vector.tensor_copy(
-                wp[:].bitcast(U16),
+                w4p[b][:].bitcast(U16),
                 w4_w[:, :, 1024 * b : 1024 * (b + 1)].bitcast(U16).rearrange("p a (m t) -> p a t m", t=4),
             )
-            ws = keep.tile([P, 2, 4, 128], U8, name="w4ps%d" % b, align_bytes=64)
+        v_s0 = keep.tile([P, S], U8, name="v_s0", align_bytes=64)
+        nc.vector.tensor_copy(v_s0[:], tab_s[:].indirect(idx[:]))
+        nc.sync.dma_start(v_s1[0:112, :].bitcast(I32), v_s0[16:128, :].bitcast(I32))
+        v_s = [v_s0, v_s1]
+        nc.sync.dma_start(tab_w[1][:], tab_words[1].rearrange("p t i -> p (t i)").bitcast(I32))
+        load_w1(0, 0)
+        for b in range(2):
+            w4ps.append(keep.tile([P, 2, 4, 128], U8, name="w4ps%d" % b, align_bytes=64))
             nc.vector.tensor_copy(
-                ws[:], w4_s[:, :, 512 * b : 512 * (b + 1)].rearrange("p a (m t) -> p a t m", t=4)
+                w4ps[b][:], w4_s[:, :, 512 * b : 512 * (b + 1)].rearrange("p a (m t) -> p a t m", t=4)
             )
-            w4p.append(wp)
-            w4ps.append(ws)
+        load_w1(0, 1)
 
         v = {}
 
@@ -115,21 +132,19 @@ def tile_list_ballot_scanner_gap_kernel(
             v[a, h] = keep.tile([P, 512], U32, name="v%d%d" % (a, h), align_bytes=64)
             nc.vector.tensor_copy(v[a, h][:], tab_w[a][:].bitcast(U32).indirect(idx[:, 32 * h : 32 * (h + 1)]))
 
-        deal_w4(0)
         gather_v(0, 0)
         gather_v(0, 1)
+        load_w1(1, 0)
+        load_w1(1, 1)
+        v2_s = share.tile([P, S2], U8, name="v2_s", align_bytes=64, offset=8 * KB)
+        nc.vector.tensor_copy(v2_s[:], tab2_s[:].indirect(idx2[:]))
         gather_v(1, 0)
         gather_v(1, 1)
-        deal_w4(1)
+        load_tab2(0)
+        load_tab2(1)
 
         g2 = keep.tile([P, 2, 4], F32, name="g2")
         nc.vector.tensor_tensor(g2[:], g[:], g[:], ALU.mult)
-        sgn = []
-        for b in range(2):
-            sgn.append(keep.tile([P, 512, 4], BF16, name="sgn%d" % b, align_bytes=64))
-            nc.scalar.activation(
-                out=sgn[b][:], in_=g[:, b : b + 1, :].to_broadcast([P, 512, 4]), func=ACT.Sign
-            )
 
         w1q, w1s = {}, {}
 
@@ -149,10 +164,10 @@ def tile_list_ballot_scanner_gap_kernel(
 
         x = {}
 
-        def stage_b(b, h):
-            x[b, h] = keep.tile([P, 4, 512], F32, name="x%d%d" % (b, h))
+        def stage_b(b, h, on_vector=0):
+            x[b, h] = share.tile([P, 4, 512], F32, name="x%d%d" % (b, h), align_bytes=64, offset=(49 + 16 * b + 8 * h) * KB)
             for t in range(4):
-                bank = psum.tile([P, 512], F32, name="bank", bufs=4)
+                bank = psum.tile([P, 512], F32, name="e_bank" if t < on_vector else "bank", bufs=4)
                 for a in range(2):
                     nc.tensor.matmul_mx(
                         out=bank[:],
@@ -163,7 +178,14 @@ def tile_list_ballot_scanner_gap_kernel(
                         start=(a == 0),
                         stop=(a == 1),
                     )
-                nc.scalar.activation(out=x[b, h][:, t, :], in_=bank[:], func=ACT.Square, scale=g[:, b, t : t + 1])
+                if t < on_vector:
+                    gb = ring.tile([P, 512], F32, name="gb")
+                    nc.vector.tensor_scalar(gb[:], bank[:], g[:, b, t : t + 1], None, ALU.mult)
+                    nc.vector.tensor_tensor(x[b, h][:, t, :], gb[:], gb[:], ALU.mult)
+                else:
+                    nc.scalar.activation(
+                        out=x[b, h][:, t, :], in_=bank[:], func=ACT.Square, scale=g[:, b, t : t + 1]
+                    )
 
         hq, hs = {}, {}
 
@@ -181,7 +203,7 @@ def tile_list_ballot_scanner_gap_kernel(
                         start=(a == 0),
                         stop=(a == 1),
                     )
-                sa = ring.tile([P, 512], F32, name="sa", bufs=4)
+                sa = ring.tile([P, 512], F32, name="sa", bufs=8)
                 nc.scalar.activation(out=sa[:, 0:n], in_=bank[:, 0:n], func=ACT.Square, scale=g[:, b, t : t + 1])
                 nc.vector.scalar_tensor_tensor(
                     out=x[b, h][:, t, cols], in0=sa[:, 0:n], scalar=g2[:, b, t : t + 1],
@@ -189,7 +211,10 @@ def tile_list_ballot_scanner_gap_kernel(
                 )
 
         def stage_h(b, h, c0, n):
-            hb = ring.tile([P, 512, 4], BF16, name="hb", align_bytes=64)
+            if c0:
+                hb = share.tile([P, n, 4], BF16, name="hb_last", align_bytes=64, offset=83 * KB)
+            else:
+                hb = ring.tile([P, 512, 4], BF16, name="hb", align_bytes=64)
             nc.scalar.activation(
                 out=hb[:, 0:n, :].rearrange("p (c i) t -> p c t i", i=4),
                 in_=x[b, h][:, :, c0 : c0 + n].rearrange("p t (c i) -> p c t i", i=4),
@@ -201,6 +226,16 @@ def tile_list_ballot_scanner_gap_kernel(
             hs[b, h, c0] = keep.tile([P, n], U8, name="hs%d%d%d" % (b, h, c0), align_bytes=64)
             nc.vector.quantize_mx(out=hq[b, h, c0][:].bitcast(FP8X4), scales=hs[b, h, c0][:], in_=flat)
 
+        v2 = {}
+
+        def gather_v2(a, half):
+            v2[a, half] = share.tile(
+                [P, 256], U32, name="v2%d%d" % (a, half), align_bytes=64, offset=(81 + 2 * half + a) * KB
+            )
+            nc.vector.tensor_copy(
+                v2[a, half][:], tab2_w[a][:].bitcast(U32).indirect(idx2[:, 16 * half : 16 * (half + 1)])
+            )
+
         stage_b(0, 0)
         stage_b(0, 1)
         quant_w1(0, 0)
@@ -208,47 +243,60 @@ def tile_list_ballot_scanner_gap_kernel(
         stage_b(1, 0)
         stage_a(0, 0, 0, 512)
         quant_w1(1, 0)
-        stage_b(1, 1)
+        stage_b(1, 1, on_vector=NV)
         quant_w1(1, 1)
+        gather_v2(0, 0)
         stage_a(0, 1, 0, 512)
+        gather_v2(1, 0)
         stage_h(0, 0, 0, 512)
         stage_a(1, 0, 0, 512)
         stage_h(0, 1, 0, 512)
-
-        v2 = []
-        for a in range(2):
-            v2.append(keep.tile([P, S2], U32, name="v2%d" % a, align_bytes=64))
-            nc.vector.tensor_copy(v2[a][:], tab2_w[a][:].bitcast(U32).indirect(idx2[:]))
-        v2_s = keep.tile([P, S2], U8, name="v2_s", align_bytes=64)
-        nc.vector.tensor_copy(v2_s[:], tab2_s[:].indirect(idx2[:]))
-
-        stage_a(1, 1, 0, 256)
+        stage_a(1, 1, 0, 512)
         stage_h(1, 0, 0, 512)
-        stage_a(1, 1, 256, 256)
         stage_h(1, 1, 0, 256)
         stage_h(1, 1, 256, 256)
+        gather_v2(0, 1)
+        gather_v2(1, 1)
 
-        pieces = [[(0, 0, 512), (1, 0, 512)], [(0, 0, 512), (1, 0, 256), (1, 256, 256)]]
+        def scores(mt, h, c0, n, on_vector):
+            m = slice(128 * mt, 128 * (mt + 1))
+            bank2 = psum.tile([P, 512], F32, name="e_bank", bufs=4)
+            parts = [(b, d0, w) for b in range(2) for (bb, hh, d0), w in widths.items()
+                     if bb == b and hh == h and d0 < c0 + n and d0 + w > c0]
+            for i, (b, d0, w) in enumerate(parts):
+                lo, hi = max(d0, c0), min(d0 + w, c0 + n)
+                nc.tensor.matmul_mx(
+                    out=bank2[:, lo - c0 : hi - c0],
+                    lhsT=v2[b, mt // 2][:, 128 * (mt % 2) : 128 * (mt % 2 + 1)].bitcast(FP8X4),
+                    lhsT_scale=v2_s[4 * b : P, m],
+                    rhs=hq[b, h, d0][:, lo - d0 : hi - d0].bitcast(FP8X4),
+                    rhs_scale=hs[b, h, d0][:, lo - d0 : hi - d0],
+                    start=(i == 0),
+                    stop=(i == len(parts) - 1),
+                )
+            dst = e[mt][:, 512 * h + c0 : 512 * h + c0 + n]
+            if on_vector:
+                nc.vector.tensor_scalar(dst, bank2[:, 0:n], hab[:, mt : mt + 1], None, ALU.mult)
+            else:
+                nc.scalar.activation(out=dst, in_=bank2[:, 0:n], func=ACT.Copy, scale=hab[:, mt : mt + 1])
+
+        widths = {(0, 0, 0): 512, (0, 1, 0): 512, (1, 0, 0): 512, (1, 1, 0): 256, (1, 1, 256): 256}
+        e = [keep.tile([P, S], F32, name="e%d" % mt) for mt in range(4)]
         for mt in range(4):
             m = slice(128 * mt, 128 * (mt + 1))
-            e = keep.tile([P, S], F32, name="e%d" % mt)
-            for h in range(2):
-                bank2 = psum.tile([P, 512], F32, name="e_bank%d" % h)
-                for i, (b, c0, n) in enumerate(pieces[h]):
-                    nc.tensor.matmul_mx(
-                        out=bank2[:, c0 : c0 + n],
-                        lhsT=v2[b][:, m].bitcast(FP8X4),
-                        lhsT_scale=v2_s[4 * b : P, m],
-                        rhs=hq[b, h, c0][:].bitcast(FP8X4),
-                        rhs_scale=hs[b, h, c0][:],
-                        start=(i == 0),
-                        stop=(i == len(pieces[h]) - 1),
-                    )
-                nc.scalar.activation(
-                    out=e[:, 512 * h : 512 * (h + 1)], in_=bank2[:], func=ACT.Copy, scale=hab[:, mt : mt + 1]
-                )
+            if mt == 0:
+                scores(mt, 0, 0, 512, True)
+                scores(mt, 1, 0, 256, True)
+                scores(mt, 1, 256, 256, False)
+            else:
+                scores(mt, 0, 0, 512, False)
+                scores(mt, 1, 0, 512, False)
             second = ring.tile([P, NP], F32, name="second")
-            nc.vector.tensor_copy(second[:], e[:].indirect(p2[:]))
-            gap = ring.tile([P, NP], F32, name="gap", bufs=4)
-            nc.vector.tensor_tensor(gap[:], e[:].indirect(p1[:]), second[:], ALU.subtract)
-            nc.sync.dma_start(out[m, :], gap[:])
+            nc.vector.tensor_copy(second[:], e[mt][:].indirect(p2[:]))
+            cuts = [0, 384, 512] if mt == 3 else [0, 512]
+            for c0, c1 in zip(cuts, cuts[1:]):
+                gap = ring.tile([P, NP], F32, name="gap", bufs=5)
+                nc.vector.tensor_tensor(
+                    gap[:, 0 : c1 - c0], e[mt][:].indirect(p1[:, c0 // 16 : c1 // 16]), second[:, c0:c1], ALU.subtract
+                )
+                nc.sync.dma_start(out[m, c0:c1], gap[:, 0 : c1 - c0])

@@ -2,7 +2,7 @@ from contextlib import ExitStack
 
 import concourse.mybir as mybir
 
-K, T, S, H, T3, S2, NP = 1024, 4096, 1024, 1024, 2048, 512, 512
+K, T, S, H, T3, S2, NPAIR = 1024, 4096, 1024, 1024, 2048, 512, 512
 FLOPS = 2 * (2 * K * H * S) + 2 * H * S2 * S
 
 F32 = mybir.dt.float32
@@ -17,7 +17,34 @@ ACT = mybir.ActivationFunctionType
 ALU = mybir.AluOpType
 
 P = 128
-NV = 2
+PACK = 4
+PASS = P * PACK
+BANK = 512
+HALF = BANK // 2
+LANES = 16
+ALIGN = 64
+KB = 1024
+
+SQUARES_ON_VECTOR = 1
+
+AT_TAB = (9 * KB, 33 * KB)
+AT_ROOT_IN = 25 * KB - 64
+AT_W4_SCALES = 25 * KB + 64
+AT_W4_WORDS = (45 * KB, 85 * KB)
+AT_TAB_SCALES = 85 * KB
+AT_W1 = {
+    (0, 0): 87 * KB,
+    (0, 1): KB + 64,
+    (1, 0): 9 * KB + 64,
+    (1, 1): 17 * KB + 64,
+}
+AT_TAB2 = (32 * KB, 40 * KB)
+AT_W4_DEALT_SCALES = (28 * KB, 48 * KB)
+AT_V2_SCALES = 2 * KB
+AT_HABIT = 3 * KB
+AT_SUMS = 49 * KB
+AT_V2 = 81 * KB
+AT_LAST_H = 83 * KB
 
 
 def tile_list_ballot_scanner_gap_kernel(
@@ -28,52 +55,70 @@ def tile_list_ballot_scanner_gap_kernel(
     with ExitStack() as ctx:
         keep = ctx.enter_context(tc.tile_pool(name="keep", bufs=1))
         ring = ctx.enter_context(tc.tile_pool(name="ring", bufs=2))
-        psum = ctx.enter_context(tc.psum_pool(name="psum", bufs=2))
+        psum = ctx.enter_context(tc.psum_pool(name="psum", bufs=8))
+        shared = ctx.enter_context(tc.tile_pool(name="shared", bufs=1))
 
-        share = ctx.enter_context(tc.tile_pool(name="share", bufs=1))
-        KB = 1024
+        def placed(shape, dtype, name, at):
+            return shared.tile(shape, dtype, name=name, align_bytes=ALIGN, offset=at)
 
-        tab_s = share.tile([P, T], U8, name="tab_s", align_bytes=64, offset=31 * KB)
-        tab2_s = keep.tile([P, T3], U8, name="tab2_s", align_bytes=64)
-        v_s1 = keep.tile([P, S], U8, name="v_s1", align_bytes=64)
-        warm = share.tile([P, 32], F32, name="warm", align_bytes=64, offset=9 * KB - 64)
+        def kept(shape, dtype, name):
+            return keep.tile(shape, dtype, name=name, align_bytes=ALIGN)
+
+        def entries(list_tile, first, count):
+            return list_tile[:, first // LANES : (first + count) // LANES]
+
+        tab_s = placed([P, T], U8, "tab_s", AT_TAB_SCALES)
+        tab2_s = kept([P, T3], U8, "tab2_s")
+        v_s1 = kept([P, S], U8, "v_s1")
+        root_in = placed([P, 48], F32, "root_in", AT_ROOT_IN)
         nc.vector.memset(tab_s[:].bitcast(I32), 0)
-        nc.vector.memset(warm[:, 0:1], 1.0)
+        nc.vector.memset(root_in[:, 0:1], 1.0)
         nc.vector.memset(v_s1[:].bitcast(I32), 0)
 
-        idx = keep.tile([P, S // 16], U16, name="idx")
+        idx = keep.tile([P, S // LANES], U16, name="idx")
         nc.sync.dma_start(idx[:], offs)
-        g = keep.tile([P, 2, 4], F32, name="g")
-        nc.sync.dma_start(g[:], gain.rearrange("(b p t) -> p b t", b=2, t=4))
-        idx2 = keep.tile([P, S2 // 16], U16, name="idx2")
+        g = keep.tile([P, 2, PACK], F32, name="g")
+        nc.sync.dma_start(g[:], gain.rearrange("(b p t) -> p b t", b=2, t=PACK))
+        idx2 = keep.tile([P, S2 // LANES], U16, name="idx2")
         nc.sync.dma_start(idx2[:], offs2)
-        w4_w = keep.tile([P, 2, 2 * H], U8, name="w4_w", align_bytes=64)
-        nc.sync.dma_start(w4_w[:].bitcast(I32), w4_words.rearrange("a p n -> p a n").bitcast(I32))
-        tab_w = []
-        for a in range(2):
-            tab_w.append(share.tile([P, T], I32, name="tab_w%d" % a, align_bytes=64, offset=(9 + 24 * a) * KB))
-        p1 = keep.tile([P, NP // 16], U16, name="p1")
+
+        w4_w = []
+
+        def load_w4_words(rb):
+            w4_w.append(placed([P, 2, 2 * PASS], U8, "w4_w%d" % rb, AT_W4_WORDS[rb]))
+            nc.sync.dma_start(
+                w4_w[rb][:].bitcast(I32),
+                w4_words[:, :, 2 * PASS * rb : 2 * PASS * (rb + 1)].rearrange("a p n -> p a n").bitcast(I32),
+            )
+
+        load_w4_words(0)
+        tab_w = [placed([P, T], I32, "tab_w%d" % kp, AT_TAB[kp]) for kp in range(2)]
+
+        def load_tab(kp):
+            nc.sync.dma_start(tab_w[kp][:], tab_words[kp].rearrange("p t i -> p (t i)").bitcast(I32))
+
+        p1 = keep.tile([P, NPAIR // LANES], U16, name="p1")
         nc.sync.dma_start(p1[:], pos1)
-        p2 = keep.tile([P, NP // 16], U16, name="p2")
+        p2 = keep.tile([P, NPAIR // LANES], U16, name="p2")
         nc.sync.dma_start(p2[:], pos2)
+
         for r in range(4):
             nc.sync.dma_start(
                 tab_s[r:P:16, :].bitcast(I32),
                 tab_scales.rearrange("a (q r) n -> r q a n", r=4)[r].bitcast(I32),
             )
-        nc.scalar.activation(out=warm[:, 1:2], in_=warm[:, 0:1], func=ACT.Sqrt)
-        sgn = []
 
-        def make_sign(b):
-            sgn.append(keep.tile([P, 512, 4], BF16, name="sgn%d" % b, align_bytes=64))
+        one = keep.tile([P, 1], F32, name="one")
+        nc.scalar.activation(out=one[:], in_=root_in[:, 0:1], func=ACT.Sqrt)
+        sign = []
+        for rb in range(2):
+            sign.append(kept([P, HALF, PACK], BF16, "sign%d" % rb))
             nc.scalar.activation(
-                out=sgn[b][:], in_=g[:, b : b + 1, :].to_broadcast([P, 512, 4]), func=ACT.Sign
+                out=sign[rb][:], in_=g[:, rb : rb + 1, :].to_broadcast([P, HALF, PACK]), func=ACT.Sign, scale=one[:]
             )
 
-        make_sign(0)
-        make_sign(1)
-        nc.sync.dma_start(tab_w[0][:], tab_words[0].rearrange("p t i -> p (t i)").bitcast(I32))
-        w4_s = share.tile([P, 2, H], U8, name="w4_s", align_bytes=64, offset=7 * KB)
+        load_tab(0)
+        w4_s = placed([P, 2, H], U8, "w4_s", AT_W4_SCALES)
         nc.vector.memset(w4_s[:].rearrange("p a n -> p (a n)").bitcast(I32), 0)
         for q in range(4):
             nc.sync.dma_start(
@@ -86,217 +131,225 @@ def tile_list_ballot_scanner_gap_kernel(
                 tab2_s[32 * q : 32 * q + 8, :].bitcast(I32),
                 tab2_scales[:, 4 * q : 4 * q + 4, :].bitcast(I32),
             )
-        hab = keep.tile([P, 4], F32, name="hab")
-        with nc.allow_non_contiguous_dma(reason="one factor a partition"):
-            nc.gpsimd.dma_start(hab[:], habit.rearrange("(c p) -> p c", p=P))
 
         w1_raw = {}
-        w1_at = {(0, 0): 25 * KB, (0, 1): 0, (1, 0): 9 * KB, (1, 1): 17 * KB}
 
-        def load_w1(b, a):
-            w1_raw[b, a] = share.tile([P, 4, 512], F32, name="w1_raw%d%d" % (b, a), align_bytes=64, offset=w1_at[b, a])
+        def load_w1(rb, kp):
+            w1_raw[rb, kp] = placed([P, PACK, PASS], F32, "w1_raw%d%d" % (rb, kp), AT_W1[rb, kp])
             nc.sync.dma_start(
-                w1_raw[b, a][:],
-                w1[512 * a : 512 * (a + 1), 512 * b : 512 * (b + 1)].rearrange("(p j) c -> p j c", j=4),
+                w1_raw[rb, kp][:],
+                w1[PASS * kp : PASS * (kp + 1), PASS * rb : PASS * (rb + 1)].rearrange("(p i) c -> p i c", i=PACK),
             )
 
         tab2_w = []
 
-        def load_tab2(a):
-            tab2_w.append(share.tile([P, T3], I32, name="tab2_w%d" % a, align_bytes=64, offset=33 * KB + 8 * KB * a))
-            nc.sync.dma_start(tab2_w[a][:], tab2_words[a].rearrange("p t i -> p (t i)").bitcast(I32))
+        def load_tab2(rb):
+            tab2_w.append(placed([P, T3], I32, "tab2_w%d" % rb, AT_TAB2[rb]))
+            nc.sync.dma_start(tab2_w[rb][:], tab2_words[rb].rearrange("p t i -> p (t i)").bitcast(I32))
 
-        w4p, w4ps = [], []
-        for b in range(2):
-            w4p.append(keep.tile([P, 2, 4, 256], U8, name="w4p%d" % b, align_bytes=64))
+        w4_codes, w4_planes = [], []
+
+        def deal_w4_words(rb):
+            w4_codes.append(kept([P, 2, PACK, 2 * P], U8, "w4_codes%d" % rb))
             nc.vector.tensor_copy(
-                w4p[b][:].bitcast(U16),
-                w4_w[:, :, 1024 * b : 1024 * (b + 1)].bitcast(U16).rearrange("p a (m t) -> p a t m", t=4),
+                w4_codes[rb][:].bitcast(U16),
+                w4_w[rb][:].bitcast(U16).rearrange("p a (m t) -> p a t m", t=PACK),
             )
-        v_s0 = keep.tile([P, S], U8, name="v_s0", align_bytes=64)
-        nc.vector.tensor_copy(v_s0[:], tab_s[:].indirect(idx[:]))
-        nc.sync.dma_start(v_s1[0:112, :].bitcast(I32), v_s0[16:128, :].bitcast(I32))
-        v_s = [v_s0, v_s1]
-        nc.sync.dma_start(tab_w[1][:], tab_words[1].rearrange("p t i -> p (t i)").bitcast(I32))
-        load_w1(0, 0)
-        for b in range(2):
-            w4ps.append(keep.tile([P, 2, 4, 128], U8, name="w4ps%d" % b, align_bytes=64))
+
+        def deal_w4_scales(rb):
+            w4_planes.append(placed([P, 2, PACK, P], U8, "w4_planes%d" % rb, AT_W4_DEALT_SCALES[rb]))
             nc.vector.tensor_copy(
-                w4ps[b][:], w4_s[:, :, 512 * b : 512 * (b + 1)].rearrange("p a (m t) -> p a t m", t=4)
+                w4_planes[rb][:],
+                w4_s[:, :, PASS * rb : PASS * (rb + 1)].rearrange("p a (m t) -> p a t m", t=PACK),
             )
-        load_w1(0, 1)
 
         v = {}
 
-        def gather_v(a, h):
-            v[a, h] = keep.tile([P, 512], U32, name="v%d%d" % (a, h), align_bytes=64)
-            nc.vector.tensor_copy(v[a, h][:], tab_w[a][:].bitcast(U32).indirect(idx[:, 32 * h : 32 * (h + 1)]))
+        def gather_v(kp, jh):
+            v[kp, jh] = kept([P, BANK], U32, "v%d%d" % (kp, jh))
+            nc.vector.tensor_copy(v[kp, jh][:], tab_w[kp][:].bitcast(U32).indirect(entries(idx, BANK * jh, BANK)))
 
+        deal_w4_words(0)
+        load_tab(1)
+        v_s0 = kept([P, S], U8, "v_s0")
+        nc.vector.tensor_copy(v_s0[:], tab_s[:].indirect(idx[:]))
+        nc.sync.dma_start(v_s1[0 : P - 16, :].bitcast(I32), v_s0[16:P, :].bitcast(I32))
+        v_s = [v_s0, v_s1]
+        load_w4_words(1)
+        load_w1(0, 0)
+        deal_w4_scales(0)
         gather_v(0, 0)
         gather_v(0, 1)
+        load_w1(0, 1)
         load_w1(1, 0)
         load_w1(1, 1)
-        v2_s = share.tile([P, S2], U8, name="v2_s", align_bytes=64, offset=8 * KB)
-        nc.vector.tensor_copy(v2_s[:], tab2_s[:].indirect(idx2[:]))
         gather_v(1, 0)
         gather_v(1, 1)
         load_tab2(0)
         load_tab2(1)
+        deal_w4_scales(1)
+        deal_w4_words(1)
 
-        g2 = keep.tile([P, 2, 4], F32, name="g2")
-        nc.vector.tensor_tensor(g2[:], g[:], g[:], ALU.mult)
+        g_sq = keep.tile([P, 2, PACK], F32, name="g_sq")
+        nc.vector.tensor_tensor(g_sq[:], g[:], g[:], ALU.mult)
 
-        w1q, w1s = {}, {}
+        w1_codes, w1_planes = {}, {}
 
-        def quant_w1(b, a):
-            wb = ring.tile([P, 4, 128, 4], BF16, name="wb", align_bytes=64)
+        def quantise_w1(rb, kp):
+            rounded = ring.tile([P, PACK, P, PACK], BF16, name="w1_rounded", align_bytes=ALIGN)
             nc.vector.tensor_copy(
-                wb[:].rearrange("p t m j -> p m j t"),
-                w1_raw[b, a][:].rearrange("p j (m t) -> p m j t", t=4),
+                rounded[:].rearrange("p t m i -> p m t i"),
+                w1_raw[rb, kp][:].rearrange("p i (m t) -> p m t i", t=PACK),
             )
-            w1q[b, a] = keep.tile([P, 512], U32, name="w1q%d%d" % (b, a), align_bytes=64)
-            w1s[b, a] = keep.tile([P, 512], U8, name="w1s%d%d" % (b, a), align_bytes=64)
+            w1_codes[rb, kp] = kept([P, PASS], U32, "w1_codes%d%d" % (rb, kp))
+            w1_planes[rb, kp] = kept([P, PASS], U8, "w1_planes%d%d" % (rb, kp))
             nc.vector.quantize_mx(
-                out=w1q[b, a][:].bitcast(FP8X4),
-                scales=w1s[b, a][:],
-                in_=wb[:].rearrange("p t m j -> p (t m j)"),
+                out=w1_codes[rb, kp][:].bitcast(FP8X4),
+                scales=w1_planes[rb, kp][:],
+                in_=rounded[:].rearrange("p t m i -> p (t m i)"),
             )
 
-        x = {}
+        def first_product(codes, planes, jh):
+            bank = psum.tile([P, BANK], F32, name="bank")
+            for kp in range(2):
+                nc.tensor.matmul_mx(
+                    out=bank[:],
+                    lhsT=codes[kp],
+                    lhsT_scale=planes[kp],
+                    rhs=v[kp, jh][:].bitcast(FP8X4),
+                    rhs_scale=v_s[kp][:, BANK * jh : BANK * (jh + 1)],
+                    start=(kp == 0),
+                    stop=(kp == 1),
+                )
+            return bank
 
-        def stage_b(b, h, on_vector=0):
-            x[b, h] = share.tile([P, 4, 512], F32, name="x%d%d" % (b, h), align_bytes=64, offset=(49 + 16 * b + 8 * h) * KB)
-            for t in range(4):
-                bank = psum.tile([P, 512], F32, name="e_bank" if t < on_vector else "bank", bufs=4)
-                for a in range(2):
-                    nc.tensor.matmul_mx(
-                        out=bank[:],
-                        lhsT=w4p[b][:, a, t, :].bitcast(FP4X4),
-                        lhsT_scale=w4ps[b][:, a, t, :],
-                        rhs=v[a, h][:].bitcast(FP8X4),
-                        rhs_scale=v_s[a][:, 512 * h : 512 * (h + 1)],
-                        start=(a == 0),
-                        stop=(a == 1),
-                    )
+        sums = {}
+
+        def square_b(rb, jh, on_vector=0):
+            sums[rb, jh] = placed([P, PACK, BANK], F32, "sums%d%d" % (rb, jh), AT_SUMS + 8 * KB * (2 * rb + jh))
+            scaled = []
+            for t in range(PACK):
+                bank = first_product(
+                    [w4_codes[rb][:, kp, t, :].bitcast(FP4X4) for kp in range(2)],
+                    [w4_planes[rb][:, kp, t, :] for kp in range(2)],
+                    jh,
+                )
                 if t < on_vector:
-                    gb = ring.tile([P, 512], F32, name="gb")
-                    nc.vector.tensor_scalar(gb[:], bank[:], g[:, b, t : t + 1], None, ALU.mult)
-                    nc.vector.tensor_tensor(x[b, h][:, t, :], gb[:], gb[:], ALU.mult)
+                    scaled.append(ring.tile([P, BANK], F32, name="b_scaled"))
+                    nc.vector.tensor_scalar(scaled[t][:], bank[:], g[:, rb, t : t + 1], None, ALU.mult)
                 else:
                     nc.scalar.activation(
-                        out=x[b, h][:, t, :], in_=bank[:], func=ACT.Square, scale=g[:, b, t : t + 1]
+                        out=sums[rb, jh][:, t, :], in_=bank[:], func=ACT.Square, scale=g[:, rb, t : t + 1]
                     )
+            for t in range(on_vector):
+                nc.vector.tensor_tensor(sums[rb, jh][:, t, :], scaled[t][:], scaled[t][:], ALU.mult)
 
-        hq, hs = {}, {}
-
-        def stage_a(b, h, c0, n):
-            cols = slice(c0, c0 + n)
-            for t in range(4):
-                bank = psum.tile([P, 512], F32, name="bank", bufs=4)
-                for a in range(2):
-                    nc.tensor.matmul_mx(
-                        out=bank[:, 0:n],
-                        lhsT=w1q[b, a][:, 128 * t : 128 * (t + 1)].bitcast(FP8X4),
-                        lhsT_scale=w1s[b, a][:, 128 * t : 128 * (t + 1)],
-                        rhs=v[a, h][:, cols].bitcast(FP8X4),
-                        rhs_scale=v_s[a][:, 512 * h + c0 : 512 * h + c0 + n],
-                        start=(a == 0),
-                        stop=(a == 1),
-                    )
-                sa = ring.tile([P, 512], F32, name="sa", bufs=8)
-                nc.scalar.activation(out=sa[:, 0:n], in_=bank[:, 0:n], func=ACT.Square, scale=g[:, b, t : t + 1])
+        def add_square_a(rb, jh):
+            for t in range(PACK):
+                cols = slice(P * t, P * (t + 1))
+                bank = first_product(
+                    [w1_codes[rb, kp][:, cols].bitcast(FP8X4) for kp in range(2)],
+                    [w1_planes[rb, kp][:, cols] for kp in range(2)],
+                    jh,
+                )
+                a_sq = ring.tile([P, BANK], F32, name="a_sq", bufs=8)
+                nc.scalar.activation(out=a_sq[:], in_=bank[:], func=ACT.Square, scale=g[:, rb, t : t + 1])
                 nc.vector.scalar_tensor_tensor(
-                    out=x[b, h][:, t, cols], in0=sa[:, 0:n], scalar=g2[:, b, t : t + 1],
-                    in1=x[b, h][:, t, cols], op0=ALU.add, op1=ALU.add,
+                    out=sums[rb, jh][:, t, :], in0=a_sq[:], scalar=g_sq[:, rb, t : t + 1],
+                    in1=sums[rb, jh][:, t, :], op0=ALU.add, op1=ALU.add,
                 )
 
-        def stage_h(b, h, c0, n):
-            if c0:
-                hb = share.tile([P, n, 4], BF16, name="hb_last", align_bytes=64, offset=83 * KB)
-            else:
-                hb = ring.tile([P, 512, 4], BF16, name="hb", align_bytes=64)
+        h_pieces = {(rb, jh): [] for rb in range(2) for jh in range(2)}
+
+        def quantise_h(rb, jh, c0, n, rounded):
             nc.scalar.activation(
-                out=hb[:, 0:n, :].rearrange("p (c i) t -> p c t i", i=4),
-                in_=x[b, h][:, :, c0 : c0 + n].rearrange("p t (c i) -> p c t i", i=4),
+                out=rounded[:, 0:n, :].rearrange("p (c i) t -> p c t i", i=4),
+                in_=sums[rb, jh][:, :, c0 : c0 + n].rearrange("p t (c i) -> p c t i", i=4),
                 func=ACT.Sqrt,
             )
-            flat = hb[:, 0:n, :].rearrange("p n t -> p (n t)")
-            nc.vector.tensor_tensor(flat, flat, sgn[b][:, 0:n, :].rearrange("p n t -> p (n t)"), ALU.mult)
-            hq[b, h, c0] = keep.tile([P, n], U32, name="hq%d%d%d" % (b, h, c0), align_bytes=64)
-            hs[b, h, c0] = keep.tile([P, n], U8, name="hs%d%d%d" % (b, h, c0), align_bytes=64)
-            nc.vector.quantize_mx(out=hq[b, h, c0][:].bitcast(FP8X4), scales=hs[b, h, c0][:], in_=flat)
+            halves = [slice(0, n // 2), slice(n // 2, n)]
+            flat = [rounded[:, s, :].rearrange("p n t -> p (n t)") for s in halves]
+            for f in flat:
+                nc.vector.tensor_tensor(f, f, sign[rb][:, 0 : n // 2, :].rearrange("p n t -> p (n t)"), ALU.mult)
+            codes = kept([P, n], U32, "h_codes%d%d%d" % (rb, jh, c0))
+            plane = kept([P, n], U8, "h_plane%d%d%d" % (rb, jh, c0))
+            for s, f in zip(halves, flat):
+                nc.vector.quantize_mx(out=codes[:, s].bitcast(FP8X4), scales=plane[:, s], in_=f)
+            h_pieces[rb, jh].append((c0, n, codes, plane))
+
+        def h_buffer():
+            return ring.tile([P, BANK, PACK], BF16, name="h_rounded", align_bytes=ALIGN)
 
         v2 = {}
 
-        def gather_v2(a, half):
-            v2[a, half] = share.tile(
-                [P, 256], U32, name="v2%d%d" % (a, half), align_bytes=64, offset=(81 + 2 * half + a) * KB
-            )
-            nc.vector.tensor_copy(
-                v2[a, half][:], tab2_w[a][:].bitcast(U32).indirect(idx2[:, 16 * half : 16 * (half + 1)])
-            )
+        def gather_v2(rb, mh):
+            v2[rb, mh] = placed([P, HALF], U32, "v2%d%d" % (rb, mh), AT_V2 + KB * (2 * mh + rb))
+            nc.vector.tensor_copy(v2[rb, mh][:], tab2_w[rb][:].bitcast(U32).indirect(entries(idx2, HALF * mh, HALF)))
 
-        stage_b(0, 0)
-        stage_b(0, 1)
-        quant_w1(0, 0)
-        quant_w1(0, 1)
-        stage_b(1, 0)
-        stage_a(0, 0, 0, 512)
-        quant_w1(1, 0)
-        stage_b(1, 1, on_vector=NV)
-        quant_w1(1, 1)
+        square_b(0, 0)
+        square_b(0, 1)
+        quantise_w1(0, 0)
+        quantise_w1(0, 1)
+        hab = placed([P, S2 // P], F32, "hab", AT_HABIT)
+        with nc.allow_non_contiguous_dma(reason="one factor a partition"):
+            nc.sync.dma_start(hab[:], habit.rearrange("(c p) -> p c", p=P))
+        square_b(1, 0)
+        add_square_a(0, 0)
+        quantise_w1(1, 0)
+        v2_s = placed([P, S2], U8, "v2_s", AT_V2_SCALES)
+        nc.vector.tensor_copy(v2_s[:], tab2_s[:].indirect(idx2[:]))
+        square_b(1, 1, on_vector=SQUARES_ON_VECTOR)
+        quantise_w1(1, 1)
         gather_v2(0, 0)
-        stage_a(0, 1, 0, 512)
+        add_square_a(0, 1)
         gather_v2(1, 0)
-        stage_h(0, 0, 0, 512)
-        stage_a(1, 0, 0, 512)
-        stage_h(0, 1, 0, 512)
-        stage_a(1, 1, 0, 512)
-        stage_h(1, 0, 0, 512)
-        stage_h(1, 1, 0, 256)
-        stage_h(1, 1, 256, 256)
+        quantise_h(0, 0, 0, BANK, h_buffer())
+        add_square_a(1, 0)
+        quantise_h(0, 1, 0, BANK, h_buffer())
+        add_square_a(1, 1)
+        quantise_h(1, 0, 0, BANK, h_buffer())
+        quantise_h(1, 1, 0, HALF, h_buffer())
+        quantise_h(1, 1, HALF, HALF, placed([P, HALF, PACK], BF16, "h_rounded_last", AT_LAST_H))
         gather_v2(0, 1)
         gather_v2(1, 1)
 
-        def scores(mt, h, c0, n, on_vector):
-            m = slice(128 * mt, 128 * (mt + 1))
-            bank2 = psum.tile([P, 512], F32, name="e_bank", bufs=4)
-            parts = [(b, d0, w) for b in range(2) for (bb, hh, d0), w in widths.items()
-                     if bb == b and hh == h and d0 < c0 + n and d0 + w > c0]
-            for i, (b, d0, w) in enumerate(parts):
-                lo, hi = max(d0, c0), min(d0 + w, c0 + n)
+        def scores(e, mt, jh, c0, n):
+            bank = psum.tile([P, BANK], F32, name="bank")
+            passes = [
+                (rb, max(d0, c0), min(d0 + w, c0 + n), d0, codes, plane)
+                for rb in range(2)
+                for d0, w, codes, plane in h_pieces[rb, jh]
+                if d0 < c0 + n and c0 < d0 + w
+            ]
+            for i, (rb, lo, hi, d0, codes, plane) in enumerate(passes):
                 nc.tensor.matmul_mx(
-                    out=bank2[:, lo - c0 : hi - c0],
-                    lhsT=v2[b, mt // 2][:, 128 * (mt % 2) : 128 * (mt % 2 + 1)].bitcast(FP8X4),
-                    lhsT_scale=v2_s[4 * b : P, m],
-                    rhs=hq[b, h, d0][:, lo - d0 : hi - d0].bitcast(FP8X4),
-                    rhs_scale=hs[b, h, d0][:, lo - d0 : hi - d0],
+                    out=bank[:, lo - c0 : hi - c0],
+                    lhsT=v2[rb, mt // 2][:, P * (mt % 2) : P * (mt % 2 + 1)].bitcast(FP8X4),
+                    lhsT_scale=v2_s[4 * rb : P, P * mt : P * (mt + 1)],
+                    rhs=codes[:, lo - d0 : hi - d0].bitcast(FP8X4),
+                    rhs_scale=plane[:, lo - d0 : hi - d0],
                     start=(i == 0),
-                    stop=(i == len(parts) - 1),
+                    stop=(i == len(passes) - 1),
                 )
-            dst = e[mt][:, 512 * h + c0 : 512 * h + c0 + n]
-            if on_vector:
-                nc.vector.tensor_scalar(dst, bank2[:, 0:n], hab[:, mt : mt + 1], None, ALU.mult)
-            else:
-                nc.scalar.activation(out=dst, in_=bank2[:, 0:n], func=ACT.Copy, scale=hab[:, mt : mt + 1])
+            nc.scalar.activation(
+                out=e[:, BANK * jh + c0 : BANK * jh + c0 + n], in_=bank[:, 0:n], func=ACT.Copy,
+                scale=hab[:, mt : mt + 1],
+            )
 
-        widths = {(0, 0, 0): 512, (0, 1, 0): 512, (1, 0, 0): 512, (1, 1, 0): 256, (1, 1, 256): 256}
-        e = [keep.tile([P, S], F32, name="e%d" % mt) for mt in range(4)]
-        for mt in range(4):
-            m = slice(128 * mt, 128 * (mt + 1))
+        e_tiles = [keep.tile([P, S], F32, name="e%d" % mt) for mt in range(S2 // P)]
+        for mt, e in enumerate(e_tiles):
+            scores(e, mt, 0, 0, BANK)
             if mt == 0:
-                scores(mt, 0, 0, 512, True)
-                scores(mt, 1, 0, 256, True)
-                scores(mt, 1, 256, 256, False)
+                scores(e, mt, 1, 0, HALF)
+                scores(e, mt, 1, HALF, HALF)
             else:
-                scores(mt, 0, 0, 512, False)
-                scores(mt, 1, 0, 512, False)
-            second = ring.tile([P, NP], F32, name="second")
-            nc.vector.tensor_copy(second[:], e[mt][:].indirect(p2[:]))
-            cuts = [0, 384, 512] if mt == 3 else [0, 512]
-            for c0, c1 in zip(cuts, cuts[1:]):
-                gap = ring.tile([P, NP], F32, name="gap", bufs=5)
+                scores(e, mt, 1, 0, BANK)
+            second = ring.tile([P, NPAIR], F32, name="second")
+            for c0 in (0, HALF):
+                nc.vector.tensor_copy(second[:, c0 : c0 + HALF], e[:].indirect(entries(p2, c0, HALF)))
+            for c0 in (0, HALF):
+                gap = ring.tile([P, HALF], F32, name="gap", bufs=8)
                 nc.vector.tensor_tensor(
-                    gap[:, 0 : c1 - c0], e[mt][:].indirect(p1[:, c0 // 16 : c1 // 16]), second[:, c0:c1], ALU.subtract
+                    gap[:], e[:].indirect(entries(p1, c0, HALF)), second[:, c0 : c0 + HALF], ALU.subtract
                 )
-                nc.sync.dma_start(out[m, c0:c1], gap[:, 0 : c1 - c0])
+                nc.sync.dma_start(out[P * mt : P * (mt + 1), c0 : c0 + HALF], gap[:])

from contextlib import ExitStack

import concourse.mybir as mybir

K, T, S, H, T3, S2, NPAIR = 1024, 4096, 1024, 1024, 2048, 512, 512
FLOPS = 2 * (2 * K * H * S) + 2 * H * S2 * S

F32 = mybir.dt.float32
BF16 = mybir.dt.bfloat16
I32 = mybir.dt.int32
U32 = mybir.dt.uint32
U16 = mybir.dt.uint16
U8 = mybir.dt.uint8
FP8X4 = mybir.dt.float8_e4m3fn_x4
FP4X4 = mybir.dt.float4_e2m1fn_x4
ACT = mybir.ActivationFunctionType
ALU = mybir.AluOpType

P = 128
PACK = 4
PASS = P * PACK
BANK = 512
HALF = BANK // 2
LANES = 16
ALIGN = 64
KB = 1024

SQUARES_ON_VECTOR = 1

AT_TAB = (9 * KB, 33 * KB)
AT_ROOT_IN = 25 * KB - 64
AT_W4_SCALES = 25 * KB + 64
AT_W4_WORDS = (45 * KB, 85 * KB)
AT_TAB_SCALES = 85 * KB
AT_W1 = {
    (0, 0): 87 * KB,
    (0, 1): KB + 64,
    (1, 0): 9 * KB + 64,
    (1, 1): 17 * KB + 64,
}
AT_TAB2 = (32 * KB, 40 * KB)
AT_W4_DEALT_SCALES = (28 * KB, 48 * KB)
AT_V2_SCALES = 2 * KB
AT_HABIT = 3 * KB
AT_SUMS = 49 * KB
AT_V2 = 81 * KB
AT_LAST_H = 83 * KB


def tile_list_ballot_scanner_gap_kernel(
    tc, tab_words, tab_scales, offs, tab2_words, tab2_scales, offs2, pos1, pos2,
    w1, w4_words, w4_scales, gain, habit, out,
):
    nc = tc.nc
    with ExitStack() as ctx:
        keep = ctx.enter_context(tc.tile_pool(name="keep", bufs=1))
        ring = ctx.enter_context(tc.tile_pool(name="ring", bufs=2))
        psum = ctx.enter_context(tc.psum_pool(name="psum", bufs=8))
        shared = ctx.enter_context(tc.tile_pool(name="shared", bufs=1))

        def placed(shape, dtype, name, at):
            return shared.tile(shape, dtype, name=name, align_bytes=ALIGN, offset=at)

        def kept(shape, dtype, name):
            return keep.tile(shape, dtype, name=name, align_bytes=ALIGN)

        def entries(list_tile, first, count):
            return list_tile[:, first // LANES : (first + count) // LANES]

        tab_s = placed([P, T], U8, "tab_s", AT_TAB_SCALES)
        tab2_s = kept([P, T3], U8, "tab2_s")
        v_s1 = kept([P, S], U8, "v_s1")
        root_in = placed([P, 48], F32, "root_in", AT_ROOT_IN)
        nc.vector.memset(tab_s[:].bitcast(I32), 0)
        nc.vector.memset(root_in[:, 0:1], 1.0)
        nc.vector.memset(v_s1[:].bitcast(I32), 0)

        idx = keep.tile([P, S // LANES], U16, name="idx")
        nc.sync.dma_start(idx[:], offs)
        g = keep.tile([P, 2, PACK], F32, name="g")
        nc.sync.dma_start(g[:], gain.rearrange("(b p t) -> p b t", b=2, t=PACK))
        idx2 = keep.tile([P, S2 // LANES], U16, name="idx2")
        nc.sync.dma_start(idx2[:], offs2)

        w4_w = []

        def load_w4_words(rb):
            w4_w.append(placed([P, 2, 2 * PASS], U8, "w4_w%d" % rb, AT_W4_WORDS[rb]))
            nc.sync.dma_start(
                w4_w[rb][:].bitcast(I32),
                w4_words[:, :, 2 * PASS * rb : 2 * PASS * (rb + 1)].rearrange("a p n -> p a n").bitcast(I32),
            )

        load_w4_words(0)
        tab_w = [placed([P, T], I32, "tab_w%d" % kp, AT_TAB[kp]) for kp in range(2)]

        def load_tab(kp):
            nc.sync.dma_start(tab_w[kp][:], tab_words[kp].rearrange("p t i -> p (t i)").bitcast(I32))

        p1 = keep.tile([P, NPAIR // LANES], U16, name="p1")
        nc.sync.dma_start(p1[:], pos1)
        p2 = keep.tile([P, NPAIR // LANES], U16, name="p2")
        nc.sync.dma_start(p2[:], pos2)

        for r in range(4):
            nc.sync.dma_start(
                tab_s[r:P:16, :].bitcast(I32),
                tab_scales.rearrange("a (q r) n -> r q a n", r=4)[r].bitcast(I32),
            )

        one = keep.tile([P, 1], F32, name="one")
        nc.scalar.activation(out=one[:], in_=root_in[:, 0:1], func=ACT.Sqrt)
        sign = []
        for rb in range(2):
            sign.append(kept([P, HALF, PACK], BF16, "sign%d" % rb))
            nc.scalar.activation(
                out=sign[rb][:], in_=g[:, rb : rb + 1, :].to_broadcast([P, HALF, PACK]), func=ACT.Sign, scale=one[:]
            )

        load_tab(0)
        w4_s = placed([P, 2, H], U8, "w4_s", AT_W4_SCALES)
        nc.vector.memset(w4_s[:].rearrange("p a n -> p (a n)").bitcast(I32), 0)
        for q in range(4):
            nc.sync.dma_start(
                w4_s[32 * q : 32 * q + 4, :, :].bitcast(I32),
                w4_scales[:, 4 * q : 4 * q + 4, :].rearrange("a r n -> r a n").bitcast(I32),
            )
        nc.gpsimd.memset(tab2_s[:].bitcast(I32), 0)
        for q in range(4):
            nc.gpsimd.dma_start(
                tab2_s[32 * q : 32 * q + 8, :].bitcast(I32),
                tab2_scales[:, 4 * q : 4 * q + 4, :].bitcast(I32),
            )

        w1_raw = {}

        def load_w1(rb, kp):
            w1_raw[rb, kp] = placed([P, PACK, PASS], F32, "w1_raw%d%d" % (rb, kp), AT_W1[rb, kp])
            nc.sync.dma_start(
                w1_raw[rb, kp][:],
                w1[PASS * kp : PASS * (kp + 1), PASS * rb : PASS * (rb + 1)].rearrange("(p i) c -> p i c", i=PACK),
            )

        tab2_w = []

        def load_tab2(rb):
            tab2_w.append(placed([P, T3], I32, "tab2_w%d" % rb, AT_TAB2[rb]))
            nc.sync.dma_start(tab2_w[rb][:], tab2_words[rb].rearrange("p t i -> p (t i)").bitcast(I32))

        w4_codes, w4_planes = [], []

        def deal_w4_words(rb):
            w4_codes.append(kept([P, 2, PACK, 2 * P], U8, "w4_codes%d" % rb))
            nc.vector.tensor_copy(
                w4_codes[rb][:].bitcast(U16),
                w4_w[rb][:].bitcast(U16).rearrange("p a (m t) -> p a t m", t=PACK),
            )

        def deal_w4_scales(rb):
            w4_planes.append(placed([P, 2, PACK, P], U8, "w4_planes%d" % rb, AT_W4_DEALT_SCALES[rb]))
            nc.vector.tensor_copy(
                w4_planes[rb][:],
                w4_s[:, :, PASS * rb : PASS * (rb + 1)].rearrange("p a (m t) -> p a t m", t=PACK),
            )

        v = {}

        def gather_v(kp, jh):
            v[kp, jh] = kept([P, BANK], U32, "v%d%d" % (kp, jh))
            nc.vector.tensor_copy(v[kp, jh][:], tab_w[kp][:].bitcast(U32).indirect(entries(idx, BANK * jh, BANK)))

        deal_w4_words(0)
        load_tab(1)
        v_s0 = kept([P, S], U8, "v_s0")
        nc.vector.tensor_copy(v_s0[:], tab_s[:].indirect(idx[:]))
        nc.sync.dma_start(v_s1[0 : P - 16, :].bitcast(I32), v_s0[16:P, :].bitcast(I32))
        v_s = [v_s0, v_s1]
        load_w4_words(1)
        load_w1(0, 0)
        deal_w4_scales(0)
        gather_v(0, 0)
        gather_v(0, 1)
        load_w1(0, 1)
        load_w1(1, 0)
        load_w1(1, 1)
        gather_v(1, 0)
        gather_v(1, 1)
        load_tab2(0)
        load_tab2(1)
        deal_w4_scales(1)
        deal_w4_words(1)

        g_sq = keep.tile([P, 2, PACK], F32, name="g_sq")
        nc.vector.tensor_tensor(g_sq[:], g[:], g[:], ALU.mult)

        w1_codes, w1_planes = {}, {}

        def quantise_w1(rb, kp):
            rounded = ring.tile([P, PACK, P, PACK], BF16, name="w1_rounded", align_bytes=ALIGN)
            nc.vector.tensor_copy(
                rounded[:].rearrange("p t m i -> p m t i"),
                w1_raw[rb, kp][:].rearrange("p i (m t) -> p m t i", t=PACK),
            )
            w1_codes[rb, kp] = kept([P, PASS], U32, "w1_codes%d%d" % (rb, kp))
            w1_planes[rb, kp] = kept([P, PASS], U8, "w1_planes%d%d" % (rb, kp))
            nc.vector.quantize_mx(
                out=w1_codes[rb, kp][:].bitcast(FP8X4),
                scales=w1_planes[rb, kp][:],
                in_=rounded[:].rearrange("p t m i -> p (t m i)"),
            )

        def first_product(codes, planes, jh):
            bank = psum.tile([P, BANK], F32, name="bank")
            for kp in range(2):
                nc.tensor.matmul_mx(
                    out=bank[:],
                    lhsT=codes[kp],
                    lhsT_scale=planes[kp],
                    rhs=v[kp, jh][:].bitcast(FP8X4),
                    rhs_scale=v_s[kp][:, BANK * jh : BANK * (jh + 1)],
                    start=(kp == 0),
                    stop=(kp == 1),
                )
            return bank

        sums = {}

        def square_b(rb, jh, on_vector=0):
            sums[rb, jh] = placed([P, PACK, BANK], F32, "sums%d%d" % (rb, jh), AT_SUMS + 8 * KB * (2 * rb + jh))
            scaled = []
            for t in range(PACK):
                bank = first_product(
                    [w4_codes[rb][:, kp, t, :].bitcast(FP4X4) for kp in range(2)],
                    [w4_planes[rb][:, kp, t, :] for kp in range(2)],
                    jh,
                )
                if t < on_vector:
                    scaled.append(ring.tile([P, BANK], F32, name="b_scaled"))
                    nc.vector.tensor_scalar(scaled[t][:], bank[:], g[:, rb, t : t + 1], None, ALU.mult)
                else:
                    nc.scalar.activation(
                        out=sums[rb, jh][:, t, :], in_=bank[:], func=ACT.Square, scale=g[:, rb, t : t + 1]
                    )
            for t in range(on_vector):
                nc.vector.tensor_tensor(sums[rb, jh][:, t, :], scaled[t][:], scaled[t][:], ALU.mult)

        def add_square_a(rb, jh):
            for t in range(PACK):
                cols = slice(P * t, P * (t + 1))
                bank = first_product(
                    [w1_codes[rb, kp][:, cols].bitcast(FP8X4) for kp in range(2)],
                    [w1_planes[rb, kp][:, cols] for kp in range(2)],
                    jh,
                )
                a_sq = ring.tile([P, BANK], F32, name="a_sq", bufs=8)
                nc.scalar.activation(out=a_sq[:], in_=bank[:], func=ACT.Square, scale=g[:, rb, t : t + 1])
                nc.vector.scalar_tensor_tensor(
                    out=sums[rb, jh][:, t, :], in0=a_sq[:], scalar=g_sq[:, rb, t : t + 1],
                    in1=sums[rb, jh][:, t, :], op0=ALU.add, op1=ALU.add,
                )

        h_pieces = {(rb, jh): [] for rb in range(2) for jh in range(2)}

        def quantise_h(rb, jh, c0, n, rounded):
            nc.scalar.activation(
                out=rounded[:, 0:n, :].rearrange("p (c i) t -> p c t i", i=4),
                in_=sums[rb, jh][:, :, c0 : c0 + n].rearrange("p t (c i) -> p c t i", i=4),
                func=ACT.Sqrt,
            )
            halves = [slice(0, n // 2), slice(n // 2, n)]
            flat = [rounded[:, s, :].rearrange("p n t -> p (n t)") for s in halves]
            for f in flat:
                nc.vector.tensor_tensor(f, f, sign[rb][:, 0 : n // 2, :].rearrange("p n t -> p (n t)"), ALU.mult)
            codes = kept([P, n], U32, "h_codes%d%d%d" % (rb, jh, c0))
            plane = kept([P, n], U8, "h_plane%d%d%d" % (rb, jh, c0))
            for s, f in zip(halves, flat):
                nc.vector.quantize_mx(out=codes[:, s].bitcast(FP8X4), scales=plane[:, s], in_=f)
            h_pieces[rb, jh].append((c0, n, codes, plane))

        def h_buffer():
            return ring.tile([P, BANK, PACK], BF16, name="h_rounded", align_bytes=ALIGN)

        v2 = {}

        def gather_v2(rb, mh):
            v2[rb, mh] = placed([P, HALF], U32, "v2%d%d" % (rb, mh), AT_V2 + KB * (2 * mh + rb))
            nc.vector.tensor_copy(v2[rb, mh][:], tab2_w[rb][:].bitcast(U32).indirect(entries(idx2, HALF * mh, HALF)))

        square_b(0, 0)
        square_b(0, 1)
        quantise_w1(0, 0)
        quantise_w1(0, 1)
        hab = placed([P, S2 // P], F32, "hab", AT_HABIT)
        with nc.allow_non_contiguous_dma(reason="one factor a partition"):
            nc.sync.dma_start(hab[:], habit.rearrange("(c p) -> p c", p=P))
        square_b(1, 0)
        add_square_a(0, 0)
        quantise_w1(1, 0)
        v2_s = placed([P, S2], U8, "v2_s", AT_V2_SCALES)
        nc.vector.tensor_copy(v2_s[:], tab2_s[:].indirect(idx2[:]))
        square_b(1, 1, on_vector=SQUARES_ON_VECTOR)
        quantise_w1(1, 1)
        gather_v2(0, 0)
        add_square_a(0, 1)
        gather_v2(1, 0)
        quantise_h(0, 0, 0, BANK, h_buffer())
        add_square_a(1, 0)
        quantise_h(0, 1, 0, BANK, h_buffer())
        add_square_a(1, 1)
        quantise_h(1, 0, 0, BANK, h_buffer())
        quantise_h(1, 1, 0, HALF, h_buffer())
        quantise_h(1, 1, HALF, HALF, placed([P, HALF, PACK], BF16, "h_rounded_last", AT_LAST_H))
        gather_v2(0, 1)
        gather_v2(1, 1)

        def scores(e, mt, jh, c0, n):
            bank = psum.tile([P, BANK], F32, name="bank")
            passes = [
                (rb, max(d0, c0), min(d0 + w, c0 + n), d0, codes, plane)
                for rb in range(2)
                for d0, w, codes, plane in h_pieces[rb, jh]
                if d0 < c0 + n and c0 < d0 + w
            ]
            for i, (rb, lo, hi, d0, codes, plane) in enumerate(passes):
                nc.tensor.matmul_mx(
                    out=bank[:, lo - c0 : hi - c0],
                    lhsT=v2[rb, mt // 2][:, P * (mt % 2) : P * (mt % 2 + 1)].bitcast(FP8X4),
                    lhsT_scale=v2_s[4 * rb : P, P * mt : P * (mt + 1)],
                    rhs=codes[:, lo - d0 : hi - d0].bitcast(FP8X4),
                    rhs_scale=plane[:, lo - d0 : hi - d0],
                    start=(i == 0),
                    stop=(i == len(passes) - 1),
                )
            nc.scalar.activation(
                out=e[:, BANK * jh + c0 : BANK * jh + c0 + n], in_=bank[:, 0:n], func=ACT.Copy,
                scale=hab[:, mt : mt + 1],
            )

        e_tiles = [keep.tile([P, S], F32, name="e%d" % mt) for mt in range(S2 // P)]
        for mt, e in enumerate(e_tiles):
            scores(e, mt, 0, 0, BANK)
            if mt == 0:
                scores(e, mt, 1, 0, HALF)
                scores(e, mt, 1, HALF, HALF)
            else:
                scores(e, mt, 1, 0, BANK)
            second = ring.tile([P, NPAIR], F32, name="second")
            for c0 in (0, HALF):
                nc.vector.tensor_copy(second[:, c0 : c0 + HALF], e[:].indirect(entries(p2, c0, HALF)))
            for c0 in (0, HALF):
                gap = ring.tile([P, HALF], F32, name="gap", bufs=8)
                nc.vector.tensor_tensor(
                    gap[:], e[:].indirect(entries(p1, c0, HALF)), second[:, c0 : c0 + HALF], ALU.subtract
                )
                nc.sync.dma_start(out[P * mt : P * (mt + 1), c0 : c0 + HALF], gap[:])
